import numpy as np
import ml_dtypes


def mxq(x, axis, fmt="e4m3"):
    dtype, down = {"e4m3": (ml_dtypes.float8_e4m3fn, 7), "e5m2": (ml_dtypes.float8_e5m2, 14)}[fmt]
    v = np.moveaxis(np.asarray(x, np.float32).astype(ml_dtypes.bfloat16).astype(np.float64), axis, -1)
    blocks = v.reshape(v.shape[:-1] + (-1, 32))
    amax = np.abs(blocks).max(-1, keepdims=True)
    byte = np.maximum(np.where(amax > 0, np.frexp(amax)[1] - 1 + 127, 0) - down, 1)
    scale = np.exp2(byte - 127.0)
    codes = (blocks / scale).astype(np.float32).astype(dtype).astype(np.float64)
    return np.moveaxis((codes * scale).reshape(v.shape), -1, axis)


WIDE = False


def mx_kscale(k):
    if not WIDE:
        return np.ones(k)
    levels = np.array([10, -10, 5, -5, 0])
    if k % 512:
        return np.exp2(np.random.permutation(np.resize(levels, k // 32))).repeat(32)
    a = np.empty((k // 512, 16))
    for p in range(k // 512):
        a[p, :8] = np.random.permutation(np.resize(levels, 8))
        for g in range(8):
            far = levels[np.abs(levels - a[p, g]) >= 10]
            a[p, g + 8] = far[np.random.randint(len(far))]
    return np.exp2(a.ravel()).repeat(32)


def f64(x):
    return np.asarray(x).astype(np.float64)


def striped(idx):
    return np.tile(idx.reshape(-1, 16).T, (8, 1)).astype(np.uint16)


def unstriped(offs):
    return offs[:16].T.reshape(-1).astype(np.int64)


E2M1 = np.array([0.0, 0.5, 1.0, 1.5, 2.0, 3.0, 4.0, 6.0, -0.0, -0.5, -1.0, -1.5, -2.0, -3.0, -4.0, -6.0])


def pack_weight(w, fmt):
    k, n = w.shape
    w = f64(np.asarray(w, np.float32).astype(ml_dtypes.bfloat16)).reshape(k // 32, 32, n)
    amax = np.abs(w).max(1)
    if fmt == "e4m3":
        byte = np.frexp(amax)[1] - 1 + 127 - 7
    else:
        mant, ex = np.frexp(amax / 6.0)
        byte = np.where(mant > 0.5, ex, ex - 1) + 127
    byte = np.clip(np.where(amax > 0, byte, 1), 1, 254)
    scaled = (w * np.exp2(127.0 - byte)[:, None, :]).reshape(k, n).astype(np.float32)
    by_word = np.ascontiguousarray(scaled.reshape(k // 512, 128, 4, n).transpose(0, 1, 3, 2))
    if fmt == "e4m3":
        words = by_word.astype(ml_dtypes.float8_e4m3fn).view(np.uint8)
    else:
        c = by_word.astype(ml_dtypes.float4_e2m1fn).view(np.uint8) & 0xF
        words = (c[..., 0::2] | (c[..., 1::2] << 4)).reshape(k // 512, 128, 2 * n)
    return np.ascontiguousarray(words), np.ascontiguousarray(byte.astype(np.uint8).reshape(k // 512, 16, n))


def unpack_weight(words, scales, fmt):
    g, _, n = scales.shape
    words = np.ascontiguousarray(words).reshape(g, 128, n, -1)
    if fmt == "e4m3":
        vals = words.view(ml_dtypes.float8_e4m3fn).astype(np.float64)
    else:
        nib = np.empty((g, 128, n, 4), np.uint8)
        nib[..., 0::2] = words & 0xF
        nib[..., 1::2] = words >> 4
        vals = E2M1[nib]
    vals = vals * np.repeat(np.exp2(scales.astype(np.float64) - 127.0), 8, axis=1)[..., None]
    return vals.transpose(0, 1, 3, 2).reshape(g * 512, n)


def gelu(v):
    return 0.5 * v * (1.0 + np.tanh(np.sqrt(2.0 / np.pi) * (v + 0.044715 * v**3)))


K, H, T, S, T2, P = 512, 1024, 4096, 1024, 2048, 1024

def setup_inputs():
    n = np.random.standard_normal
    s = mx_kscale(K)[:, None]
    u = mx_kscale(H)[:, None]
    tab_words, tab_scales = pack_weight(n((K, T)) * s, "e4m3")
    w2_words, w2_scales = pack_weight(n((K, H)) / np.sqrt(K) / s * u.T, "e2m1")
    return {
        "tab_words": tab_words, "tab_scales": tab_scales,
        "offs": striped(np.random.permutation(T)[:S]),
        "w1": (n((K, H)) / np.sqrt(K) / s * u.T).astype(np.float32),
        "w2_words": w2_words, "w2_scales": w2_scales,
        "page0": (n((H, T2)) * u).astype(np.float32),
        "wgs": np.exp(0.3 * n((128, S))).astype(np.float32),
        "offs2": striped(np.random.permutation(T2)[:S]),
        "offs3": striped(np.random.permutation(T2)[:P]),
        "gm": n((H, P)).astype(np.float32),
        "w3": (n((H, H)) / np.sqrt(H) / u * u.T).astype(np.float32),
        "wgo": np.exp(0.3 * n((128, P))).astype(np.float32),
        "offs4": striped(np.random.permutation(T2)[:P]),
    }

def reference(tab_words, tab_scales, offs, w1, w2_words, w2_scales, page0, wgs, offs2, offs3, gm, w3, wgo, offs4):
    v = unpack_weight(tab_words, tab_scales, "e4m3")[:, unstriped(offs)]
    w2 = unpack_weight(w2_words, w2_scales, "e2m1")
    a = mxq(f64(w1), 0, "e4m3").T @ v
    b = w2.T @ v
    h = a + np.abs(a - b)
    page = f64(page0).copy()
    page[:, unstriped(offs2)] = np.tile(f64(wgs), (H // 128, 1)) * h
    x = page[:, unstriped(offs3)]
    xm = x * f64(gm)
    y0 = mxq(f64(w3), 0, "e4m3").T @ mxq(xm, 0, "e4m3")
    y = np.maximum(y0, x)
    page[:, unstriped(offs4)] = np.tile(f64(wgo), (H // 128, 1)) * y
    return page

@@ -1,0 +1,312 @@
+from contextlib import ExitStack
+
+import concourse.mybir as mybir
+from concourse.masks import make_identity
+
+K, H, T, S, T2 = 512, 1024, 4096, 1024, 2048
+FLOPS = 2 * K * H * S * 2 + 2 * H * H * S
+
+F32 = mybir.dt.float32
+BF16 = mybir.dt.bfloat16
+I32 = mybir.dt.int32
+U32 = mybir.dt.uint32
+U16 = mybir.dt.uint16
+U8 = mybir.dt.uint8
+FP8X4 = mybir.dt.float8_e4m3fn_x4
+FP4X4 = mybir.dt.float4_e2m1fn_x4
+ACT = mybir.ActivationFunctionType
+MULT = mybir.AluOpType.mult
+ADD = mybir.AluOpType.add
+MAX = mybir.AluOpType.max
+
+P = 128
+PACK = 4
+PASS = P * PACK
+GROUPS = H // PASS
+TILES = H // P
+HALF = 512
+HALVES = S // HALF
+LIST_COLS = HALF // 16
+QUADS = 4
+QUAD = P // QUADS
+
+
+def skewed(lead):
+    steps = []
+    for n in range(TILES + lead):
+        if n < TILES:
+            steps.append((n, 0))
+        if n >= lead:
+            steps.append((n - lead, 1))
+    return steps
+
+
+def tile_list_mould_breakout_page_kernel(
+    tc, tab_words, tab_scales, offs, w1, w2_words, w2_scales, page0, wgs, offs2, offs3, gm, w3, wgo, offs4, out
+):
+    nc = tc.nc
+    with ExitStack() as ctx:
+        keep = ctx.enter_context(tc.tile_pool(name="keep", bufs=1))
+        ring = ctx.enter_context(tc.tile_pool(name="ring", bufs=2))
+        shared = ctx.enter_context(tc.tile_pool(name="shared", bufs=1))
+        first = ctx.enter_context(tc.tile_pool(name="first", bufs=1))
+        psum = ctx.enter_context(tc.psum_pool(name="psum", bufs=1))
+
+        page0_rows = page0.rearrange("(g p t) c -> g t p c", p=P, t=PACK)
+        out_rows = out.rearrange("(g p t) c -> g t p c", p=P, t=PACK)
+        gm_rows = gm.rearrange("(g p t) j -> g p t j", p=P, t=PACK)
+        wgs_rows = wgs.rearrange("(q t) j -> q t j", t=PACK)
+        wgo_rows = wgo.rearrange("(q t) j -> q t j", t=PACK)
+
+        def half(h):
+            return slice(h * HALF, (h + 1) * HALF)
+
+        def list_half(lst, h):
+            return lst[:, h * LIST_COLS : (h + 1) * LIST_COLS]
+
+        def load_list(src, name):
+            lst = keep.tile([P, S // 16], U16, name=name)
+            nc.sync.dma_start(lst[:], src)
+            return lst
+
+        def load_scale_rows(plane, src):
+            nc.vector.memset(plane[:].bitcast(I32), 0)
+            for q in range(QUADS):
+                nc.gpsimd.dma_start(
+                    plane[QUAD * q : QUAD * q + 4, :].bitcast(I32), src[4 * q : 4 * q + 4, :].bitcast(I32)
+                )
+
+        def load_weight_block(rows, g):
+            raw = ring.tile([P, PACK, PASS], F32, name="w_raw", tag="w_raw")
+            nc.sync.dma_start(raw[:], rows.rearrange("(p j) c -> p j c", j=PACK)[:, :, g * PASS : (g + 1) * PASS])
+            return raw
+
+        def quantise_weight_block(raw, g, codes, scales):
+            words = ring.tile([P, PASS * PACK], BF16, name="w_bf", tag="w_bf", bufs=3, align_bytes=64)
+            src = raw[:].rearrange("p j (m t) -> p m t j", t=PACK)
+            dst = words[:].rearrange("p (t m j) -> p m t j", t=PACK, j=PACK)
+            for u in range(2):
+                nc.scalar.activation(dst[:, :, 2 * u : 2 * u + 2, :], src[:, :, 2 * u : 2 * u + 2, :], ACT.Copy)
+                cols = slice(g * PASS + 2 * u * P, g * PASS + 2 * (u + 1) * P)
+                nc.vector.quantize_mx(
+                    out=codes[:, cols].bitcast(FP8X4),
+                    scales=scales[:, cols],
+                    in_=words[:, 2 * u * P * PACK : 2 * (u + 1) * P * PACK],
+                )
+
+        w2_raw = keep.tile([P, 2 * H], U8, name="w2_raw")
+        nc.sync.dma_start(w2_raw[:].bitcast(I32), w2_words[0].bitcast(I32))
+        tab = keep.tile([P, T], U32, name="tab", tag="tab_wgo")
+        nc.sync.dma_start(tab[:].bitcast(I32), tab_words[0].rearrange("p n t -> p (n t)").bitcast(I32))
+        idx1 = load_list(offs, "idx1")
+        tab_plane = ring.tile([P, T], U8, name="tab_plane", tag="w_bf", bufs=3, align_bytes=64)
+        load_scale_rows(tab_plane, tab_scales[0])
+        w2_scale_raw = keep.tile([P, H], U8, name="w2_scale_raw")
+        load_scale_rows(w2_scale_raw, w2_scales[0])
+        w1_raw = load_weight_block(w1, 0)
+        idx2 = load_list(offs2, "idx2")
+
+        wgs_sb = shared.tile([P, PACK, S], F32, name="wgs_sb", offset=0)
+        pages = [keep.tile([P, T2], F32, name=f"page{i}") for i in range(TILES)]
+
+        def load_page(i):
+            g, t = divmod(i, PACK)
+            if g == 0:
+                for q in range(QUADS):
+                    nc.sync.dma_start(wgs_sb[QUAD * q : QUAD * (q + 1), t, :], wgs_rows[:, t, :])
+            nc.sync.dma_start(pages[i][:], page0_rows[g, t])
+
+        load_page(0)
+        load_page(1)
+
+        ident = keep.tile([P, P], F32, name="ident")
+        make_identity(nc, ident[:])
+
+        w2_codes = keep.tile([P, 2 * H], U8, name="w2_codes", align_bytes=64)
+        nc.vector.tensor_copy(
+            w2_codes[:].rearrange("p (g t m b) -> p g t m b", g=GROUPS, t=PACK, b=2),
+            w2_raw[:].rearrange("p (g m t b) -> p g t m b", g=GROUPS, t=PACK, b=2),
+        )
+        w2_plane = keep.tile([P, H], U8, name="w2_plane", align_bytes=64)
+        nc.vector.tensor_copy(
+            w2_plane[:].rearrange("p (g t m) -> p g t m", g=GROUPS, t=PACK),
+            w2_scale_raw[:].rearrange("p (g m t) -> p g t m", g=GROUPS, t=PACK),
+        )
+
+        v_codes = keep.tile([P, S], U32, name="v_codes", tag="words0", align_bytes=64)
+        v_plane = keep.tile([P, S], U8, name="v_plane", align_bytes=64)
+        for h in range(HALVES):
+            nc.vector.tensor_copy(v_codes[:, half(h)], tab[:].indirect(list_half(idx1, h)))
+            nc.vector.tensor_copy(v_plane[:, half(h)], tab_plane[:].indirect(list_half(idx1, h)))
+
+        w1_codes = keep.tile([P, H], U32, name="w1_codes", tag="words1", align_bytes=64)
+        w1_plane = keep.tile([P, H], U8, name="w1_plane", align_bytes=64)
+        quantise_weight_block(w1_raw, 0, w1_codes, w1_plane)
+
+        w3_codes = [keep.tile([P, H], U32, name=f"w3_codes{g}", align_bytes=64) for g in range(GROUPS)]
+        w3_plane = [keep.tile([P, H], U8, name=f"w3_plane{g}", align_bytes=64) for g in range(GROUPS)]
+
+        def bank(tag):
+            return psum.tile([P, HALF], F32, name=tag, tag=tag, bufs=4)
+
+        def staged(name, bufs=2):
+            return ring.tile([P, HALF], F32, name=name, tag=name, bufs=bufs)
+
+        def turned_sum(*terms):
+            acc = bank("tr")
+            for c in range(HALF // P):
+                cols = slice(c * P, (c + 1) * P)
+                for n, term in enumerate(terms):
+                    nc.tensor.matmul(
+                        acc[:, cols], term[:, cols], ident[:],
+                        start=(n == 0), stop=(n == len(terms) - 1), is_transpose=True,
+                    )
+            return acc
+
+        def write_columns(page, lst, base, other, func, scale, factors):
+            diff = turned_sum(base, other)
+            f_turned = staged("f_turned")
+            nc.scalar.activation(f_turned[:], diff[:], func, scale=scale)
+            back = turned_sum(f_turned[:])
+            result = staged("result", bufs=6)
+            nc.scalar.copy(result[:], back[:])
+            nc.gpsimd.tensor_tensor(result[:], result[:], base, ADD)
+            nc.gpsimd.tensor_tensor(result[:], result[:], factors, MULT)
+            nc.vector.tensor_copy(page[:].indirect(lst), result[:])
+
+        def first_writing(i, h):
+            cols = slice(i * P, (i + 1) * P)
+            a_bank = bank("mm")
+            nc.tensor.matmul_mx(
+                out=a_bank[:], lhsT=w1_codes[:, cols].bitcast(FP8X4), lhsT_scale=w1_plane[:, cols],
+                rhs=v_codes[:, half(h)].bitcast(FP8X4), rhs_scale=v_plane[:, half(h)], start=True, stop=True,
+            )
+            b_bank = bank("mm")
+            nc.tensor.matmul_mx(
+                out=b_bank[:], lhsT=w2_codes[:, 2 * i * P : 2 * (i + 1) * P].bitcast(FP4X4),
+                lhsT_scale=w2_plane[:, cols],
+                rhs=v_codes[:, half(h)].bitcast(FP8X4), rhs_scale=v_plane[:, half(h)], start=True, stop=True,
+            )
+            negated = staged("negated")
+            if (i, h) == (0, 0):
+                nc.scalar.activation(negated[:], b_bank[:], ACT.Copy, scale=-1.0)
+                result = staged("result", bufs=6)
+                nc.vector.tensor_tensor(result[:], a_bank[:], negated[:], ADD)
+                nc.vector.scalar_tensor_tensor(negated[:], result[:], -1.0, result[:], MULT, MAX)
+                nc.vector.tensor_tensor(result[:], a_bank[:], negated[:], ADD)
+                nc.vector.tensor_tensor(result[:], result[:], wgs_sb[:, 0, half(0)], MULT)
+                nc.vector.tensor_copy(pages[0][:].indirect(list_half(idx2, 0)), result[:])
+                return
+            a = staged("a", bufs=4)
+            nc.scalar.copy(a[:], a_bank[:])
+            nc.scalar.activation(negated[:], b_bank[:], ACT.Copy, scale=-1.0)
+            write_columns(
+                pages[i], list_half(idx2, h), a[:], negated[:], ACT.Abs, 1.0, wgs_sb[:, i % PACK, half(h)]
+            )
+
+        gm_sb = {}
+        planes = {}
+        picked = {}
+
+        def load_gm(g, h):
+            gm_sb[g, h] = keep.tile([P, PACK, HALF], F32, name="gm_sb", tag=f"gm{g}")
+            nc.sync.dma_start(gm_sb[g, h][:], gm_rows[g][:, :, half(h)])
+
+        def pick(i, h):
+            nc.vector.tensor_copy(picked[i, h], pages[i][:].indirect(list_half(idx3, h)))
+
+        def weigh(i, h):
+            g, t = divmod(i, PACK)
+            if t == 0 and h == 0:
+                planes[g, h] = shared.tile([P, PACK, HALF], BF16, name=f"planes{g}", offset=(2 + g) * PASS * 8)
+            if t == 0 and h == 1:
+                planes[g, h] = keep.tile([P, PACK, HALF], BF16, name="planes", tag=f"words{g}", align_bytes=64)
+            nc.gpsimd.tensor_tensor(planes[g, h][:, t, :], picked[i, h], gm_sb[g, h][:, t, :], MULT)
+
+        xm_codes = {}
+        xm_plane = {}
+
+        def quantise_xm(g, h):
+            if h == 0:
+                words = ring.tile([P, HALF, PACK], BF16, name="xm_words", tag="w_bf", bufs=3, align_bytes=64)
+            else:
+                words = first.tile([P, HALF, PACK], BF16, name=f"xm_words{g}", offset=g * HALF * 8, align_bytes=64)
+            nc.scalar.copy(words[:], planes[g, h][:].rearrange("p t c -> p c t"))
+            xm_codes[g, h] = keep.tile([P, HALF], U32, name=f"xm_codes{g}{h}", align_bytes=64)
+            xm_plane[g, h] = keep.tile([P, HALF], U8, name=f"xm_plane{g}{h}", align_bytes=64)
+            nc.vector.quantize_mx(
+                out=xm_codes[g, h][:].bitcast(FP8X4), scales=xm_plane[g, h][:],
+                in_=words[:].rearrange("p c t -> p (c t)"),
+            )
+
+        idx3 = load_list(offs3, "idx3")
+        for i in range(TILES):
+            picked[i, 0] = first.tile([P, HALF], F32, name=f"picked0{i}", offset=i * HALF * 4, align_bytes=64)[:]
+        weight_blocks = [(w1, 1, w1_codes, w1_plane)] + [
+            (w3[g * PASS : (g + 1) * PASS, :], gc, w3_codes[g], w3_plane[g])
+            for gc in range(GROUPS)
+            for g in range(GROUPS)
+        ]
+        for i, h in skewed(1):
+            first_writing(i, h)
+            if h == 0 and i + 2 < TILES:
+                load_page(i + 2)
+            if h == 1:
+                pick(i, 0)
+                if i < len(weight_blocks):
+                    rows, gc, codes, scales = weight_blocks[i]
+                    quantise_weight_block(load_weight_block(rows, gc), gc, codes, scales)
+                if i == PACK:
+                    load_gm(0, 0)
+                    load_gm(1, 0)
+                    idx4 = load_list(offs4, "idx4")
+                    wgo_sb = keep.tile([P, PACK, S], F32, name="wgo_sb", tag="tab_wgo")
+                    for q in range(QUADS):
+                        nc.sync.dma_start(wgo_sb[QUAD * q : QUAD * (q + 1), :, :], wgo_rows)
+
+        for g in range(GROUPS):
+            for t in range(PACK):
+                weigh(g * PACK + t, 0)
+            quantise_xm(g, 0)
+
+        for g in range(GROUPS):
+            picked1 = shared.tile([P, PACK, HALF], F32, name=f"picked1{g}", offset=g * PACK * HALF * 4)
+            for t in range(PACK):
+                picked[g * PACK + t, 1] = picked1[:, t, :]
+                pick(g * PACK + t, 1)
+        for g in range(GROUPS):
+            load_gm(g, 1)
+
+        def second_writing(i, h):
+            cols = slice(i * P, (i + 1) * P)
+            y0_bank = bank("mm")
+            for g in range(GROUPS):
+                nc.tensor.matmul_mx(
+                    out=y0_bank[:], lhsT=w3_codes[g][:, cols].bitcast(FP8X4), lhsT_scale=w3_plane[g][:, cols],
+                    rhs=xm_codes[g, h][:].bitcast(FP8X4), rhs_scale=xm_plane[g, h][:],
+                    start=(g == 0), stop=(g == GROUPS - 1),
+                )
+            if (i, h) == (0, 0):
+                result = staged("result", bufs=6)
+                nc.vector.tensor_tensor(result[:], y0_bank[:], picked[0, 0], MAX)
+                nc.vector.tensor_tensor(result[:], result[:], wgo_sb[:, 0, half(0)], MULT)
+                nc.vector.tensor_copy(pages[0][:].indirect(list_half(idx4, 0)), result[:])
+                return
+            negated = staged("negated")
+            nc.scalar.activation(negated[:], y0_bank[:], ACT.Copy, scale=-1.0)
+            write_columns(
+                pages[i], list_half(idx4, h), picked[i, h], negated[:], ACT.Relu, -1.0,
+                wgo_sb[:, i % PACK, half(h)],
+            )
+            if h == 1:
+                nc.sync.dma_start(out_rows[i // PACK, i % PACK], pages[i][:])
+
+        for i in range(TILES):
+            second_writing(i, 0)
+            if i == 1:
+                for n in range(TILES):
+                    weigh(n, 1)
+            if i in (1, 3):
+                quantise_xm(i // 2, 1)
+        for i in range(TILES):
+            second_writing(i, 1)

@@ -81,29 +81,27 @@ def tile_list_mould_breakout_page_kernel(
             nc.sync.dma_start(raw[:], rows.rearrange("(p j) c -> p j c", j=PACK)[:, :, g * PASS : (g + 1) * PASS])
             return raw
 
-        def quantise_weight_block(raw, g, codes, scales):
-            words = ring.tile([P, PASS * PACK], BF16, name="w_bf", tag="w_bf", bufs=3, align_bytes=64)
+        def round_and_deal(words, raw, first_t, n_t):
             src = raw[:].rearrange("p j (m t) -> p m t j", t=PACK)
-            dst = words[:].rearrange("p (t m j) -> p m t j", t=PACK, j=PACK)
-            for u in range(2):
-                nc.scalar.activation(dst[:, :, 2 * u : 2 * u + 2, :], src[:, :, 2 * u : 2 * u + 2, :], ACT.Copy)
-                cols = slice(g * PASS + 2 * u * P, g * PASS + 2 * (u + 1) * P)
-                nc.vector.quantize_mx(
-                    out=codes[:, cols].bitcast(FP8X4),
-                    scales=scales[:, cols],
-                    in_=words[:, 2 * u * P * PACK : 2 * (u + 1) * P * PACK],
-                )
+            dst = words.rearrange("p (t m j) -> p m t j", t=PACK, j=PACK)
+            nc.scalar.activation(dst[:, :, first_t : first_t + n_t, :], src[:, :, first_t : first_t + n_t, :], ACT.Copy)
+
+        def quantise(codes, scales, words):
+            nc.vector.quantize_mx(out=codes.bitcast(FP8X4), scales=scales, in_=words)
+
+        def staged_words(name):
+            return ring.tile([P, H * PACK], BF16, name=name, tag="w_bf", align_bytes=64)
 
         w2_raw = keep.tile([P, 2 * H], U8, name="w2_raw")
         nc.sync.dma_start(w2_raw[:].bitcast(I32), w2_words[0].bitcast(I32))
         tab = keep.tile([P, T], U32, name="tab", tag="tab_wgo")
         nc.sync.dma_start(tab[:].bitcast(I32), tab_words[0].rearrange("p n t -> p (n t)").bitcast(I32))
         idx1 = load_list(offs, "idx1")
-        tab_plane = ring.tile([P, T], U8, name="tab_plane", tag="w_bf", bufs=3, align_bytes=64)
+        tab_plane = keep.tile([P, T], U8, name="tab_plane", tag="words1", align_bytes=64)
         load_scale_rows(tab_plane, tab_scales[0])
-        w2_scale_raw = keep.tile([P, H], U8, name="w2_scale_raw")
+        w2_scale_raw = keep.tile([P, H], U8, name="w2_scale_raw", tag="w1_plane", align_bytes=64)
         load_scale_rows(w2_scale_raw, w2_scales[0])
-        w1_raw = load_weight_block(w1, 0)
+        w1_raw = [load_weight_block(w1, g) for g in range(GROUPS)]
         idx2 = load_list(offs2, "idx2")
 
         wgs_sb = shared.tile([P, PACK, S], F32, name="wgs_sb", offset=0)
@@ -140,20 +138,27 @@ def tile_list_mould_breakout_page_kernel(
             nc.vector.tensor_copy(v_plane[:, half(h)], tab_plane[:].indirect(list_half(idx1, h)))
 
         w1_codes = keep.tile([P, H], U32, name="w1_codes", tag="words1", align_bytes=64)
-        w1_plane = keep.tile([P, H], U8, name="w1_plane", align_bytes=64)
-        quantise_weight_block(w1_raw, 0, w1_codes, w1_plane)
+        w1_plane = keep.tile([P, H], U8, name="w1_plane", tag="w1_plane", align_bytes=64)
+        w1_words = staged_words("w1_words")
+        for u in range(2):
+            round_and_deal(w1_words[:, : PASS * PACK], w1_raw[0], 2 * u, 2)
+            cols = slice(2 * u * P, 2 * (u + 1) * P)
+            quantise(w1_codes[:, cols], w1_plane[:, cols], w1_words[:, 2 * u * PASS : 2 * (u + 1) * PASS])
+        for u in range(2):
+            round_and_deal(w1_words[:, PASS * PACK :], w1_raw[1], 2 * u, 2)
+        quantise(w1_codes[:, PASS:], w1_plane[:, PASS:], w1_words[:, PASS * PACK :])
 
         w3_codes = [keep.tile([P, H], U32, name=f"w3_codes{g}", align_bytes=64) for g in range(GROUPS)]
         w3_plane = [keep.tile([P, H], U8, name=f"w3_plane{g}", align_bytes=64) for g in range(GROUPS)]
 
-        def bank(tag):
-            return psum.tile([P, HALF], F32, name=tag, tag=tag, bufs=4)
+        def bank_pair():
+            return psum.tile([P, 2, HALF], F32, name="pair", tag="pair", bufs=2)
 
         def staged(name, bufs=2):
             return ring.tile([P, HALF], F32, name=name, tag=name, bufs=bufs)
 
-        def turned_sum(*terms):
-            acc = bank("tr")
+        def turned_sum(tag, *terms):
+            acc = psum.tile([P, HALF], F32, name=tag, tag=tag, bufs=2)
             for c in range(HALF // P):
                 cols = slice(c * P, (c + 1) * P)
                 for n, term in enumerate(terms):
@@ -163,45 +168,60 @@ def tile_list_mould_breakout_page_kernel(
                     )
             return acc
 
-        def write_columns(page, lst, base, other, func, scale, factors):
-            diff = turned_sum(base, other)
-            f_turned = staged("f_turned")
+        def write_columns(page, lst, base, other, func, scale, factors, last=False):
+            diff = turned_sum("diff", base, other)
+            f_turned = staged("f_turned", bufs=3)
             nc.scalar.activation(f_turned[:], diff[:], func, scale=scale)
-            back = turned_sum(f_turned[:])
-            result = staged("result", bufs=6)
+            back = turned_sum("back", f_turned[:])
+            if last:
+                result = shared.tile([P, HALF], F32, name="last_result", offset=PACK * S * 4)
+            else:
+                result = staged("result", bufs=6)
             nc.scalar.copy(result[:], back[:])
             nc.gpsimd.tensor_tensor(result[:], result[:], base, ADD)
             nc.gpsimd.tensor_tensor(result[:], result[:], factors, MULT)
             nc.vector.tensor_copy(page[:].indirect(lst), result[:])
 
+        def write_directly(i, lst, result, factors):
+            if i == 0:
+                nc.vector.tensor_tensor(pages[i][:].indirect(lst), result[:], factors, MULT)
+            else:
+                nc.vector.tensor_tensor(result[:], result[:], factors, MULT)
+                nc.vector.tensor_copy(pages[i][:].indirect(lst), result[:])
+
         def first_writing(i, h):
             cols = slice(i * P, (i + 1) * P)
-            a_bank = bank("mm")
+            direct = h == 0 and i < 2
+            if direct:
+                tag = ("diff", "back")[i]
+                a_bank, b_bank = [psum.tile([P, HALF], F32, name=tag, tag=tag, bufs=2)[:] for n in range(2)]
+            else:
+                pair = bank_pair()
+                a_bank, b_bank = pair[:, 0, :], pair[:, 1, :]
             nc.tensor.matmul_mx(
-                out=a_bank[:], lhsT=w1_codes[:, cols].bitcast(FP8X4), lhsT_scale=w1_plane[:, cols],
+                out=a_bank, lhsT=w1_codes[:, cols].bitcast(FP8X4), lhsT_scale=w1_plane[:, cols],
                 rhs=v_codes[:, half(h)].bitcast(FP8X4), rhs_scale=v_plane[:, half(h)], start=True, stop=True,
             )
-            b_bank = bank("mm")
             nc.tensor.matmul_mx(
-                out=b_bank[:], lhsT=w2_codes[:, 2 * i * P : 2 * (i + 1) * P].bitcast(FP4X4),
+                out=b_bank, lhsT=w2_codes[:, 2 * i * P : 2 * (i + 1) * P].bitcast(FP4X4),
                 lhsT_scale=w2_plane[:, cols],
                 rhs=v_codes[:, half(h)].bitcast(FP8X4), rhs_scale=v_plane[:, half(h)], start=True, stop=True,
             )
-            negated = staged("negated")
-            if (i, h) == (0, 0):
-                nc.scalar.activation(negated[:], b_bank[:], ACT.Copy, scale=-1.0)
+            negated = staged("negated", bufs=3)
+            if direct:
+                nc.scalar.activation(negated[:], b_bank, ACT.Copy, scale=-1.0)
                 result = staged("result", bufs=6)
-                nc.vector.tensor_tensor(result[:], a_bank[:], negated[:], ADD)
+                nc.vector.tensor_tensor(result[:], a_bank, negated[:], ADD)
                 nc.vector.scalar_tensor_tensor(negated[:], result[:], -1.0, result[:], MULT, MAX)
-                nc.vector.tensor_tensor(result[:], a_bank[:], negated[:], ADD)
-                nc.vector.tensor_tensor(result[:], result[:], wgs_sb[:, 0, half(0)], MULT)
-                nc.vector.tensor_copy(pages[0][:].indirect(list_half(idx2, 0)), result[:])
+                nc.vector.tensor_tensor(result[:], a_bank, negated[:], ADD)
+                write_directly(i, list_half(idx2, 0), result, wgs_sb[:, i, half(0)])
                 return
             a = staged("a", bufs=4)
-            nc.scalar.copy(a[:], a_bank[:])
-            nc.scalar.activation(negated[:], b_bank[:], ACT.Copy, scale=-1.0)
+            nc.scalar.copy(a[:], a_bank)
+            nc.scalar.activation(negated[:], b_bank, ACT.Copy, scale=-1.0)
             write_columns(
-                pages[i], list_half(idx2, h), a[:], negated[:], ACT.Abs, 1.0, wgs_sb[:, i % PACK, half(h)]
+                pages[i], list_half(idx2, h), a[:], negated[:], ACT.Abs, 1.0, wgs_sb[:, i % PACK, half(h)],
+                last=(i, h) == (TILES - 1, 1),
             )
 
         gm_sb = {}
@@ -209,7 +229,7 @@ def tile_list_mould_breakout_page_kernel(
         picked = {}
 
         def load_gm(g, h):
-            gm_sb[g, h] = keep.tile([P, PACK, HALF], F32, name="gm_sb", tag=f"gm{g}")
+            gm_sb[g, h] = ring.tile([P, PACK, HALF], F32, name="gm_sb", tag="gm" if h == 0 else "w_raw")
             nc.sync.dma_start(gm_sb[g, h][:], gm_rows[g][:, :, half(h)])
 
         def pick(i, h):
@@ -218,7 +238,7 @@ def tile_list_mould_breakout_page_kernel(
         def weigh(i, h):
             g, t = divmod(i, PACK)
             if t == 0 and h == 0:
-                planes[g, h] = shared.tile([P, PACK, HALF], BF16, name=f"planes{g}", offset=(2 + g) * PASS * 8)
+                planes[g, h] = shared.tile([P, PACK, HALF], BF16, name=f"planes{g}", offset=g * PASS * 8)
             if t == 0 and h == 1:
                 planes[g, h] = keep.tile([P, PACK, HALF], BF16, name="planes", tag=f"words{g}", align_bytes=64)
             nc.gpsimd.tensor_tensor(planes[g, h][:, t, :], picked[i, h], gm_sb[g, h][:, t, :], MULT)
@@ -226,74 +246,87 @@ def tile_list_mould_breakout_page_kernel(
         xm_codes = {}
         xm_plane = {}
 
-        def quantise_xm(g, h):
-            if h == 0:
-                words = ring.tile([P, HALF, PACK], BF16, name="xm_words", tag="w_bf", bufs=3, align_bytes=64)
-            else:
-                words = first.tile([P, HALF, PACK], BF16, name=f"xm_words{g}", offset=g * HALF * 8, align_bytes=64)
-            nc.scalar.copy(words[:], planes[g, h][:].rearrange("p t c -> p c t"))
-            xm_codes[g, h] = keep.tile([P, HALF], U32, name=f"xm_codes{g}{h}", align_bytes=64)
-            xm_plane[g, h] = keep.tile([P, HALF], U8, name=f"xm_plane{g}{h}", align_bytes=64)
-            nc.vector.quantize_mx(
-                out=xm_codes[g, h][:].bitcast(FP8X4), scales=xm_plane[g, h][:],
-                in_=words[:].rearrange("p c t -> p (c t)"),
+        def quantise_xm(h, words):
+            for g in range(GROUPS):
+                for u in range(2):
+                    cols = slice(u * HALF // 2, (u + 1) * HALF // 2)
+                    nc.scalar.copy(words[:, g, cols, :], planes[g, h][:, :, cols].rearrange("p t c -> p c t"))
+            xm_codes[h] = keep.tile([P, GROUPS, HALF], U32, name=f"xm_codes{h}", align_bytes=64)
+            xm_plane[h] = keep.tile([P, GROUPS, HALF], U8, name=f"xm_plane{h}", align_bytes=64)
+            quantise(
+                xm_codes[h][:].rearrange("p g c -> p (g c)"), xm_plane[h][:].rearrange("p g c -> p (g c)"),
+                words[:].rearrange("p g c t -> p (g c t)"),
             )
 
         idx3 = load_list(offs3, "idx3")
         for i in range(TILES):
             picked[i, 0] = first.tile([P, HALF], F32, name=f"picked0{i}", offset=i * HALF * 4, align_bytes=64)[:]
-        weight_blocks = [(w1, 1, w1_codes, w1_plane)] + [
-            (w3[g * PASS : (g + 1) * PASS, :], gc, w3_codes[g], w3_plane[g])
-            for gc in range(GROUPS)
-            for g in range(GROUPS)
-        ]
+
+        def quantise_w3(g):
+            words = staged_words("w3_words")
+            for gc in range(GROUPS):
+                raw = load_weight_block(w3[g * PASS : (g + 1) * PASS, :], gc)
+                for u in range(2):
+                    round_and_deal(words[:, gc * PASS * PACK : (gc + 1) * PASS * PACK], raw, 2 * u, 2)
+            quantise(w3_codes[g][:], w3_plane[g][:], words[:])
+
         for i, h in skewed(1):
             first_writing(i, h)
-            if h == 0 and i + 2 < TILES:
-                load_page(i + 2)
             if h == 1:
                 pick(i, 0)
-                if i < len(weight_blocks):
-                    rows, gc, codes, scales = weight_blocks[i]
-                    quantise_weight_block(load_weight_block(rows, gc), gc, codes, scales)
-                if i == PACK:
-                    load_gm(0, 0)
-                    load_gm(1, 0)
-                    idx4 = load_list(offs4, "idx4")
-                    wgo_sb = keep.tile([P, PACK, S], F32, name="wgo_sb", tag="tab_wgo")
-                    for q in range(QUADS):
-                        nc.sync.dma_start(wgo_sb[QUAD * q : QUAD * (q + 1), :, :], wgo_rows)
+                continue
+            if i == 0:
+                quantise_w3(0)
+            if i + 2 < TILES:
+                load_page(i + 2)
+            if i == 3:
+                quantise_w3(1)
+            if i + 2 == TILES - 1:
+                idx4 = load_list(offs4, "idx4")
+                wgo_sb = keep.tile([P, PACK, S], F32, name="wgo_sb", tag="tab_wgo")
+                for q in range(QUADS):
+                    nc.sync.dma_start(wgo_sb[QUAD * q : QUAD * (q + 1), :, :], wgo_rows)
+                for hh in range(HALVES):
+                    for g in range(GROUPS):
+                        load_gm(g, hh)
+
+        for i in range(TILES):
+            weigh(i, 0)
+        quantise_xm(0, ring.tile([P, GROUPS, HALF, PACK], BF16, name="xm_words0", tag="w_bf", align_bytes=64))
 
         for g in range(GROUPS):
-            for t in range(PACK):
-                weigh(g * PACK + t, 0)
-            quantise_xm(g, 0)
-
-        for g in range(GROUPS):
-            picked1 = shared.tile([P, PACK, HALF], F32, name=f"picked1{g}", offset=g * PACK * HALF * 4)
+            picked1 = shared.tile([P, PACK, HALF], F32, name=f"picked1{g}", offset=(1 - g) * 5 * HALF * 4)
             for t in range(PACK):
                 picked[g * PACK + t, 1] = picked1[:, t, :]
                 pick(g * PACK + t, 1)
-        for g in range(GROUPS):
-            load_gm(g, 1)
 
-        def second_writing(i, h):
+        y0_banks = {}
+
+        def second_product(i, h, y0_bank):
             cols = slice(i * P, (i + 1) * P)
-            y0_bank = bank("mm")
             for g in range(GROUPS):
                 nc.tensor.matmul_mx(
-                    out=y0_bank[:], lhsT=w3_codes[g][:, cols].bitcast(FP8X4), lhsT_scale=w3_plane[g][:, cols],
-                    rhs=xm_codes[g, h][:].bitcast(FP8X4), rhs_scale=xm_plane[g, h][:],
+                    out=y0_bank, lhsT=w3_codes[g][:, cols].bitcast(FP8X4), lhsT_scale=w3_plane[g][:, cols],
+                    rhs=xm_codes[h][:, g, :].bitcast(FP8X4), rhs_scale=xm_plane[h][:, g, :],
                     start=(g == 0), stop=(g == GROUPS - 1),
                 )
-            if (i, h) == (0, 0):
+            y0_banks[i, h] = y0_bank
+
+        def second_writing(i, h):
+            if h == 0 and i < 2:
+                second_product(i, h, psum.tile([P, HALF], F32, name="back", tag="back", bufs=2)[:])
+            elif i % 2 == 0:
+                pair = bank_pair()
+                for n in range(2):
+                    second_product(i + n, h, pair[:, n, :])
+            y0_bank = y0_banks[i, h]
+            if h == 0 and i < 2:
                 result = staged("result", bufs=6)
-                nc.vector.tensor_tensor(result[:], y0_bank[:], picked[0, 0], MAX)
-                nc.vector.tensor_tensor(result[:], result[:], wgo_sb[:, 0, half(0)], MULT)
-                nc.vector.tensor_copy(pages[0][:].indirect(list_half(idx4, 0)), result[:])
+                nc.vector.tensor_tensor(result[:], y0_bank, picked[i, 0], MAX)
+                write_directly(i, list_half(idx4, 0), result, wgo_sb[:, i, half(0)])
                 return
-            negated = staged("negated")
-            nc.scalar.activation(negated[:], y0_bank[:], ACT.Copy, scale=-1.0)
+            negated = staged("negated", bufs=3)
+            nc.scalar.activation(negated[:], y0_bank, ACT.Copy, scale=-1.0)
             write_columns(
                 pages[i], list_half(idx4, h), picked[i, h], negated[:], ACT.Relu, -1.0,
                 wgo_sb[:, i % PACK, half(h)],
@@ -303,10 +336,9 @@ def tile_list_mould_breakout_page_kernel(
 
         for i in range(TILES):
             second_writing(i, 0)
-            if i == 1:
+            if i == 2:
                 for n in range(TILES):
                     weigh(n, 1)
-            if i in (1, 3):
-                quantise_xm(i // 2, 1)
+                quantise_xm(1, ring.tile([P, GROUPS, HALF, PACK], BF16, name="xm_words1", tag="w_bf", align_bytes=64))
         for i in range(TILES):
             second_writing(i, 1)

from contextlib import ExitStack

import concourse.mybir as mybir
from concourse.masks import make_identity

K, H, T, S, T2 = 512, 1024, 4096, 1024, 2048
FLOPS = 2 * K * H * S * 2 + 2 * H * H * S

F32 = mybir.dt.float32
BF16 = mybir.dt.bfloat16
I32 = mybir.dt.int32
U32 = mybir.dt.uint32
U16 = mybir.dt.uint16
U8 = mybir.dt.uint8
FP8X4 = mybir.dt.float8_e4m3fn_x4
FP4X4 = mybir.dt.float4_e2m1fn_x4
ACT = mybir.ActivationFunctionType
MULT = mybir.AluOpType.mult
ADD = mybir.AluOpType.add
MAX = mybir.AluOpType.max

P = 128
PACK = 4
PASS = P * PACK
GROUPS = H // PASS
TILES = H // P
HALF = 512
HALVES = S // HALF
LIST_COLS = HALF // 16
QUADS = 4
QUAD = P // QUADS


def skewed(lead):
    steps = []
    for n in range(TILES + lead):
        if n < TILES:
            steps.append((n, 0))
        if n >= lead:
            steps.append((n - lead, 1))
    return steps


def tile_list_mould_breakout_page_kernel(
    tc, tab_words, tab_scales, offs, w1, w2_words, w2_scales, page0, wgs, offs2, offs3, gm, w3, wgo, offs4, out
):
    nc = tc.nc
    with ExitStack() as ctx:
        keep = ctx.enter_context(tc.tile_pool(name="keep", bufs=1))
        ring = ctx.enter_context(tc.tile_pool(name="ring", bufs=2))
        shared = ctx.enter_context(tc.tile_pool(name="shared", bufs=1))
        first = ctx.enter_context(tc.tile_pool(name="first", bufs=1))
        psum = ctx.enter_context(tc.psum_pool(name="psum", bufs=1))

        page0_rows = page0.rearrange("(g p t) c -> g t p c", p=P, t=PACK)
        out_rows = out.rearrange("(g p t) c -> g t p c", p=P, t=PACK)
        gm_rows = gm.rearrange("(g p t) j -> g p t j", p=P, t=PACK)
        wgs_rows = wgs.rearrange("(q t) j -> q t j", t=PACK)
        wgo_rows = wgo.rearrange("(q t) j -> q t j", t=PACK)

        def half(h):
            return slice(h * HALF, (h + 1) * HALF)

        def list_half(lst, h):
            return lst[:, h * LIST_COLS : (h + 1) * LIST_COLS]

        def load_list(src, name):
            lst = keep.tile([P, S // 16], U16, name=name)
            nc.sync.dma_start(lst[:], src)
            return lst

        def load_scale_rows(plane, src):
            nc.vector.memset(plane[:].bitcast(I32), 0)
            for q in range(QUADS):
                nc.gpsimd.dma_start(
                    plane[QUAD * q : QUAD * q + 4, :].bitcast(I32), src[4 * q : 4 * q + 4, :].bitcast(I32)
                )

        def load_weight_block(rows, g):
            raw = ring.tile([P, PACK, PASS], F32, name="w_raw", tag="w_raw")
            nc.sync.dma_start(raw[:], rows.rearrange("(p j) c -> p j c", j=PACK)[:, :, g * PASS : (g + 1) * PASS])
            return raw

        def round_and_deal(words, raw, first_t, n_t):
            src = raw[:].rearrange("p j (m t) -> p m t j", t=PACK)
            dst = words.rearrange("p (t m j) -> p m t j", t=PACK, j=PACK)
            nc.scalar.activation(dst[:, :, first_t : first_t + n_t, :], src[:, :, first_t : first_t + n_t, :], ACT.Copy)

        def quantise(codes, scales, words):
            nc.vector.quantize_mx(out=codes.bitcast(FP8X4), scales=scales, in_=words)

        def staged_words(name):
            return ring.tile([P, H * PACK], BF16, name=name, tag="w_bf", align_bytes=64)

        w2_raw = keep.tile([P, 2 * H], U8, name="w2_raw")
        nc.sync.dma_start(w2_raw[:].bitcast(I32), w2_words[0].bitcast(I32))
        tab = keep.tile([P, T], U32, name="tab", tag="tab_wgo")
        nc.sync.dma_start(tab[:].bitcast(I32), tab_words[0].rearrange("p n t -> p (n t)").bitcast(I32))
        idx1 = load_list(offs, "idx1")
        tab_plane = keep.tile([P, T], U8, name="tab_plane", tag="words1", align_bytes=64)
        load_scale_rows(tab_plane, tab_scales[0])
        w2_scale_raw = keep.tile([P, H], U8, name="w2_scale_raw", tag="w1_plane", align_bytes=64)
        load_scale_rows(w2_scale_raw, w2_scales[0])
        w1_raw = [load_weight_block(w1, g) for g in range(GROUPS)]
        idx2 = load_list(offs2, "idx2")

        wgs_sb = shared.tile([P, PACK, S], F32, name="wgs_sb", offset=0)
        pages = [keep.tile([P, T2], F32, name=f"page{i}") for i in range(TILES)]

        def load_page(i):
            g, t = divmod(i, PACK)
            if g == 0:
                for q in range(QUADS):
                    nc.sync.dma_start(wgs_sb[QUAD * q : QUAD * (q + 1), t, :], wgs_rows[:, t, :])
            nc.sync.dma_start(pages[i][:], page0_rows[g, t])

        load_page(0)
        load_page(1)

        ident = keep.tile([P, P], F32, name="ident")
        make_identity(nc, ident[:])

        w2_codes = keep.tile([P, 2 * H], U8, name="w2_codes", align_bytes=64)
        nc.vector.tensor_copy(
            w2_codes[:].rearrange("p (g t m b) -> p g t m b", g=GROUPS, t=PACK, b=2),
            w2_raw[:].rearrange("p (g m t b) -> p g t m b", g=GROUPS, t=PACK, b=2),
        )
        w2_plane = keep.tile([P, H], U8, name="w2_plane", align_bytes=64)
        nc.vector.tensor_copy(
            w2_plane[:].rearrange("p (g t m) -> p g t m", g=GROUPS, t=PACK),
            w2_scale_raw[:].rearrange("p (g m t) -> p g t m", g=GROUPS, t=PACK),
        )

        v_codes = keep.tile([P, S], U32, name="v_codes", tag="words0", align_bytes=64)
        v_plane = keep.tile([P, S], U8, name="v_plane", align_bytes=64)
        for h in range(HALVES):
            nc.vector.tensor_copy(v_codes[:, half(h)], tab[:].indirect(list_half(idx1, h)))
            nc.vector.tensor_copy(v_plane[:, half(h)], tab_plane[:].indirect(list_half(idx1, h)))

        w1_codes = keep.tile([P, H], U32, name="w1_codes", tag="words1", align_bytes=64)
        w1_plane = keep.tile([P, H], U8, name="w1_plane", tag="w1_plane", align_bytes=64)
        w1_words = staged_words("w1_words")
        for u in range(2):
            round_and_deal(w1_words[:, : PASS * PACK], w1_raw[0], 2 * u, 2)
            cols = slice(2 * u * P, 2 * (u + 1) * P)
            quantise(w1_codes[:, cols], w1_plane[:, cols], w1_words[:, 2 * u * PASS : 2 * (u + 1) * PASS])
        for u in range(2):
            round_and_deal(w1_words[:, PASS * PACK :], w1_raw[1], 2 * u, 2)
        quantise(w1_codes[:, PASS:], w1_plane[:, PASS:], w1_words[:, PASS * PACK :])

        w3_codes = [keep.tile([P, H], U32, name=f"w3_codes{g}", align_bytes=64) for g in range(GROUPS)]
        w3_plane = [keep.tile([P, H], U8, name=f"w3_plane{g}", align_bytes=64) for g in range(GROUPS)]

        def bank_pair():
            return psum.tile([P, 2, HALF], F32, name="pair", tag="pair", bufs=2)

        def staged(name, bufs=2):
            return ring.tile([P, HALF], F32, name=name, tag=name, bufs=bufs)

        def turned_sum(tag, *terms):
            acc = psum.tile([P, HALF], F32, name=tag, tag=tag, bufs=2)
            for c in range(HALF // P):
                cols = slice(c * P, (c + 1) * P)
                for n, term in enumerate(terms):
                    nc.tensor.matmul(
                        acc[:, cols], term[:, cols], ident[:],
                        start=(n == 0), stop=(n == len(terms) - 1), is_transpose=True,
                    )
            return acc

        def write_columns(page, lst, base, other, func, scale, factors, last=False):
            diff = turned_sum("diff", base, other)
            f_turned = staged("f_turned", bufs=3)
            nc.scalar.activation(f_turned[:], diff[:], func, scale=scale)
            back = turned_sum("back", f_turned[:])
            if last:
                result = shared.tile([P, HALF], F32, name="last_result", offset=PACK * S * 4)
            else:
                result = staged("result", bufs=6)
            nc.scalar.copy(result[:], back[:])
            nc.gpsimd.tensor_tensor(result[:], result[:], base, ADD)
            nc.gpsimd.tensor_tensor(result[:], result[:], factors, MULT)
            nc.vector.tensor_copy(page[:].indirect(lst), result[:])

        def write_directly(i, lst, result, factors):
            if i == 0:
                nc.vector.tensor_tensor(pages[i][:].indirect(lst), result[:], factors, MULT)
            else:
                nc.vector.tensor_tensor(result[:], result[:], factors, MULT)
                nc.vector.tensor_copy(pages[i][:].indirect(lst), result[:])

        def first_writing(i, h):
            cols = slice(i * P, (i + 1) * P)
            direct = h == 0 and i < 2
            if direct:
                tag = ("diff", "back")[i]
                a_bank, b_bank = [psum.tile([P, HALF], F32, name=tag, tag=tag, bufs=2)[:] for n in range(2)]
            else:
                pair = bank_pair()
                a_bank, b_bank = pair[:, 0, :], pair[:, 1, :]
            nc.tensor.matmul_mx(
                out=a_bank, lhsT=w1_codes[:, cols].bitcast(FP8X4), lhsT_scale=w1_plane[:, cols],
                rhs=v_codes[:, half(h)].bitcast(FP8X4), rhs_scale=v_plane[:, half(h)], start=True, stop=True,
            )
            nc.tensor.matmul_mx(
                out=b_bank, lhsT=w2_codes[:, 2 * i * P : 2 * (i + 1) * P].bitcast(FP4X4),
                lhsT_scale=w2_plane[:, cols],
                rhs=v_codes[:, half(h)].bitcast(FP8X4), rhs_scale=v_plane[:, half(h)], start=True, stop=True,
            )
            negated = staged("negated", bufs=3)
            if direct:
                nc.scalar.activation(negated[:], b_bank, ACT.Copy, scale=-1.0)
                result = staged("result", bufs=6)
                nc.vector.tensor_tensor(result[:], a_bank, negated[:], ADD)
                nc.vector.scalar_tensor_tensor(negated[:], result[:], -1.0, result[:], MULT, MAX)
                nc.vector.tensor_tensor(result[:], a_bank, negated[:], ADD)
                write_directly(i, list_half(idx2, 0), result, wgs_sb[:, i, half(0)])
                return
            a = staged("a", bufs=4)
            nc.scalar.copy(a[:], a_bank)
            nc.scalar.activation(negated[:], b_bank, ACT.Copy, scale=-1.0)
            write_columns(
                pages[i], list_half(idx2, h), a[:], negated[:], ACT.Abs, 1.0, wgs_sb[:, i % PACK, half(h)],
                last=(i, h) == (TILES - 1, 1),
            )

        gm_sb = {}
        planes = {}
        picked = {}

        def load_gm(g, h):
            gm_sb[g, h] = ring.tile([P, PACK, HALF], F32, name="gm_sb", tag="gm" if h == 0 else "w_raw")
            nc.sync.dma_start(gm_sb[g, h][:], gm_rows[g][:, :, half(h)])

        def pick(i, h):
            nc.vector.tensor_copy(picked[i, h], pages[i][:].indirect(list_half(idx3, h)))

        def weigh(i, h):
            g, t = divmod(i, PACK)
            if t == 0 and h == 0:
                planes[g, h] = shared.tile([P, PACK, HALF], BF16, name=f"planes{g}", offset=g * PASS * 8)
            if t == 0 and h == 1:
                planes[g, h] = keep.tile([P, PACK, HALF], BF16, name="planes", tag=f"words{g}", align_bytes=64)
            nc.gpsimd.tensor_tensor(planes[g, h][:, t, :], picked[i, h], gm_sb[g, h][:, t, :], MULT)

        xm_codes = {}
        xm_plane = {}

        def quantise_xm(h, words):
            for g in range(GROUPS):
                for u in range(2):
                    cols = slice(u * HALF // 2, (u + 1) * HALF // 2)
                    nc.scalar.copy(words[:, g, cols, :], planes[g, h][:, :, cols].rearrange("p t c -> p c t"))
            xm_codes[h] = keep.tile([P, GROUPS, HALF], U32, name=f"xm_codes{h}", align_bytes=64)
            xm_plane[h] = keep.tile([P, GROUPS, HALF], U8, name=f"xm_plane{h}", align_bytes=64)
            quantise(
                xm_codes[h][:].rearrange("p g c -> p (g c)"), xm_plane[h][:].rearrange("p g c -> p (g c)"),
                words[:].rearrange("p g c t -> p (g c t)"),
            )

        idx3 = load_list(offs3, "idx3")
        for i in range(TILES):
            picked[i, 0] = first.tile([P, HALF], F32, name=f"picked0{i}", offset=i * HALF * 4, align_bytes=64)[:]

        def quantise_w3(g):
            words = staged_words("w3_words")
            for gc in range(GROUPS):
                raw = load_weight_block(w3[g * PASS : (g + 1) * PASS, :], gc)
                for u in range(2):
                    round_and_deal(words[:, gc * PASS * PACK : (gc + 1) * PASS * PACK], raw, 2 * u, 2)
            quantise(w3_codes[g][:], w3_plane[g][:], words[:])

        for i, h in skewed(1):
            first_writing(i, h)
            if h == 1:
                pick(i, 0)
                continue
            if i == 0:
                quantise_w3(0)
            if i + 2 < TILES:
                load_page(i + 2)
            if i == 3:
                quantise_w3(1)
            if i + 2 == TILES - 1:
                idx4 = load_list(offs4, "idx4")
                wgo_sb = keep.tile([P, PACK, S], F32, name="wgo_sb", tag="tab_wgo")
                for q in range(QUADS):
                    nc.sync.dma_start(wgo_sb[QUAD * q : QUAD * (q + 1), :, :], wgo_rows)
                for hh in range(HALVES):
                    for g in range(GROUPS):
                        load_gm(g, hh)

        for i in range(TILES):
            weigh(i, 0)
        quantise_xm(0, ring.tile([P, GROUPS, HALF, PACK], BF16, name="xm_words0", tag="w_bf", align_bytes=64))

        for g in range(GROUPS):
            picked1 = shared.tile([P, PACK, HALF], F32, name=f"picked1{g}", offset=(1 - g) * 5 * HALF * 4)
            for t in range(PACK):
                picked[g * PACK + t, 1] = picked1[:, t, :]
                pick(g * PACK + t, 1)

        y0_banks = {}

        def second_product(i, h, y0_bank):
            cols = slice(i * P, (i + 1) * P)
            for g in range(GROUPS):
                nc.tensor.matmul_mx(
                    out=y0_bank, lhsT=w3_codes[g][:, cols].bitcast(FP8X4), lhsT_scale=w3_plane[g][:, cols],
                    rhs=xm_codes[h][:, g, :].bitcast(FP8X4), rhs_scale=xm_plane[h][:, g, :],
                    start=(g == 0), stop=(g == GROUPS - 1),
                )
            y0_banks[i, h] = y0_bank

        def second_writing(i, h):
            if h == 0 and i < 2:
                second_product(i, h, psum.tile([P, HALF], F32, name="back", tag="back", bufs=2)[:])
            elif i % 2 == 0:
                pair = bank_pair()
                for n in range(2):
                    second_product(i + n, h, pair[:, n, :])
            y0_bank = y0_banks[i, h]
            if h == 0 and i < 2:
                result = staged("result", bufs=6)
                nc.vector.tensor_tensor(result[:], y0_bank, picked[i, 0], MAX)
                write_directly(i, list_half(idx4, 0), result, wgo_sb[:, i, half(0)])
                return
            negated = staged("negated", bufs=3)
            nc.scalar.activation(negated[:], y0_bank, ACT.Copy, scale=-1.0)
            write_columns(
                pages[i], list_half(idx4, h), picked[i, h], negated[:], ACT.Relu, -1.0,
                wgo_sb[:, i % PACK, half(h)],
            )
            if h == 1:
                nc.sync.dma_start(out_rows[i // PACK, i % PACK], pages[i][:])

        for i in range(TILES):
            second_writing(i, 0)
            if i == 2:
                for n in range(TILES):
                    weigh(n, 1)
                quantise_xm(1, ring.tile([P, GROUPS, HALF, PACK], BF16, name="xm_words1", tag="w_bf", align_bytes=64))
        for i in range(TILES):
            second_writing(i, 1)
